import numpy as np
import ml_dtypes


def mxq(x, axis, fmt="e4m3"):
    dtype, down = {"e4m3": (ml_dtypes.float8_e4m3fn, 7), "e5m2": (ml_dtypes.float8_e5m2, 14)}[fmt]
    v = np.moveaxis(np.asarray(x, np.float32).astype(ml_dtypes.bfloat16).astype(np.float64), axis, -1)
    blocks = v.reshape(v.shape[:-1] + (-1, 32))
    amax = np.abs(blocks).max(-1, keepdims=True)
    byte = np.maximum(np.where(amax > 0, np.frexp(amax)[1] - 1 + 127, 0) - down, 1)
    scale = np.exp2(byte - 127.0)
    codes = (blocks / scale).astype(np.float32).astype(dtype).astype(np.float64)
    return np.moveaxis((codes * scale).reshape(v.shape), -1, axis)


WIDE = False


def mx_kscale(k):
    if not WIDE:
        return np.ones(k)
    levels = np.array([18, -18])
    if k % 512:
        return np.exp2(np.random.permutation(np.resize(levels, k // 32))).repeat(32)
    a = np.empty((k // 512, 16))
    for p in range(k // 512):
        a[p, :8] = np.random.permutation(np.resize(levels, 8))
        for g in range(8):
            far = levels[np.abs(levels - a[p, g]) >= 10]
            a[p, g + 8] = far[np.random.randint(len(far))]
    return np.exp2(a.ravel()).repeat(32)


def f64(x):
    return np.asarray(x).astype(np.float64)


def striped(idx):
    return np.tile(np.asarray(idx).reshape(-1, 16).T, (8, 1)).astype(np.uint16)


def unstriped(offs):
    return offs[:16].T.reshape(-1).astype(np.int64)


E2M1 = np.array([0.0, 0.5, 1.0, 1.5, 2.0, 3.0, 4.0, 6.0, -0.0, -0.5, -1.0, -1.5, -2.0, -3.0, -4.0, -6.0])


def pack_weight(w, fmt):
    k, n = w.shape
    w = f64(np.asarray(w, np.float32).astype(ml_dtypes.bfloat16)).reshape(k // 32, 32, n)
    amax = np.abs(w).max(1)
    if fmt == "e4m3":
        byte = np.frexp(amax)[1] - 1 + 127 - 7
    else:
        mant, ex = np.frexp(amax / 6.0)
        byte = np.where(mant > 0.5, ex, ex - 1) + 127
    byte = np.clip(np.where(amax > 0, byte, 1), 1, 254)
    scaled = (w * np.exp2(127.0 - byte)[:, None, :]).reshape(k, n).astype(np.float32)
    by_word = np.ascontiguousarray(scaled.reshape(k // 512, 128, 4, n).transpose(0, 1, 3, 2))
    if fmt == "e4m3":
        words = by_word.astype(ml_dtypes.float8_e4m3fn).view(np.uint8)
    else:
        c = by_word.astype(ml_dtypes.float4_e2m1fn).view(np.uint8) & 0xF
        words = (c[..., 0::2] | (c[..., 1::2] << 4)).reshape(k // 512, 128, 2 * n)
    return np.ascontiguousarray(words), np.ascontiguousarray(byte.astype(np.uint8).reshape(k // 512, 16, n))


def unpack_weight(words, scales, fmt):
    g, _, n = scales.shape
    words = np.ascontiguousarray(words).reshape(g, 128, n, -1)
    if fmt == "e4m3":
        vals = words.view(ml_dtypes.float8_e4m3fn).astype(np.float64)
    else:
        nib = np.empty((g, 128, n, 4), np.uint8)
        nib[..., 0::2] = words & 0xF
        nib[..., 1::2] = words >> 4
        vals = E2M1[nib]
    vals = vals * np.repeat(np.exp2(scales.astype(np.float64) - 127.0), 8, axis=1)[..., None]
    return vals.transpose(0, 1, 3, 2).reshape(g * 512, n)


B, N, T, D, R = 1, 512, 2048, 1024, 512


def setup_inputs():
    n = np.random.standard_normal
    idx = np.random.permutation(T)[:B * N]
    s = mx_kscale(D)[:, None]
    z = mx_kscale(R)[:, None]
    q = n((B, D, R))
    do = n((B, D, R))
    cp = pack_weight(n((D, T)) * (0.50 / np.sqrt(D)) / s, "e2m1")
    return {
        "qT": (q * s).astype(np.float32),
        "c_words": np.ascontiguousarray(cp[0].reshape(1, 2, 128, T, 2).transpose(0, 2, 3, 1, 4)).reshape(1, 128, T, 4),
        "c_scales": cp[1],
        "doT": (do * s).astype(np.float32),
        "lse": (np.log(N) + 0.12 + 0.1 * n((B, R, 1))).astype(np.float32),
        "delta": (0.3 * n((B, R, 1))).astype(np.float32),
        "rw": (np.random.uniform(0.5, 1.5, (B, R, 1)) * N / np.sqrt(R) * z).astype(np.float32),
        "qm": (q.transpose(0, 2, 1) / z).astype(np.float32),
        "dom": (do.transpose(0, 2, 1) / z).astype(np.float32),
        "offs": striped(idx),
    }


def reference(qT, c_words, c_scales, doT, lse, delta, rw, qm, dom, offs):
    idx = unstriped(offs)
    c = unpack_weight(c_words.reshape(1, 128, T, 2, 2).transpose(0, 3, 1, 2, 4).reshape(2, 128, 2 * T), c_scales, "e2m1")
    pick = lambda x: x[:, idx].reshape(x.shape[0], B, N).transpose(1, 0, 2)
    cq = pick(c)
    a = mxq(f64(qT), 1, "e4m3").transpose(0, 2, 1) @ cq
    p = np.exp(a - f64(lse))
    dp = mxq(f64(doT), 1, "e5m2").transpose(0, 2, 1) @ cq
    ds = f64(rw) * p * (dp - f64(delta))
    dk = mxq(f64(qm), 1, "e4m3").transpose(0, 2, 1) @ mxq(ds, 1, "e5m2")
    dv = mxq(f64(dom), 1, "e5m2").transpose(0, 2, 1) @ mxq(f64(rw) * p, 1, "e4m3")
    gc = np.zeros((D, T))
    gc[:, idx] = (dk + dv).transpose(1, 0, 2).reshape(D, B * N)
    return gc

@@ -1,0 +1,200 @@
+from contextlib import ExitStack
+
+import concourse.mybir as mybir
+
+N, T, D, R = 512, 2048, 1024, 512
+FLOPS = 4 * 2 * R * N * D
+
+F32 = mybir.dt.float32
+BF16 = mybir.dt.bfloat16
+I32 = mybir.dt.int32
+U32 = mybir.dt.uint32
+U16 = mybir.dt.uint16
+U8 = mybir.dt.uint8
+E4M3 = mybir.dt.float8_e4m3fn_x4
+E5M2 = mybir.dt.float8_e5m2_x4
+E2M1 = mybir.dt.float4_e2m1fn_x4
+ALU = mybir.AluOpType
+ACT = mybir.ActivationFunctionType
+
+P = 128
+PACK = 4
+PASSES = D // (P * PACK)
+TILES = D // P
+WINDOWS = 3
+
+
+def tile_attend_gat_lse_c_kernel(tc, qT, c_words, c_scales, doT, lse, delta, rw, qm, dom, offs, out):
+    nc = tc.nc
+
+    def copy_on(engine, dst, src):
+        if engine == "vector":
+            nc.vector.tensor_copy(out=dst, in_=src)
+        else:
+            nc.scalar.copy(out=dst, in_=src)
+
+    def weave(engine, dst, src):
+        copy_on(engine, dst.rearrange("p (c i) t -> p c t i", i=4), src.rearrange("p t (c i) -> p c t i", i=4))
+
+    def deal(engine, dst, src):
+        copy_on(engine, dst.rearrange("p j s t -> p s t j"), src.rearrange("p t (s j) -> p s t j", j=PACK))
+
+    with ExitStack() as ctx:
+        keep = ctx.enter_context(tc.tile_pool(name="keep", bufs=1))
+        psum = ctx.enter_context(tc.psum_pool(name="psum", bufs=1))
+
+        def sbuf(shape, dtype, name):
+            return keep.tile(shape, dtype, name=name, align_bytes=64)
+
+        def quantised(name, width):
+            return sbuf([P, width], U32, name + "_codes"), sbuf([P, width], U8, name + "_scales")
+
+        def quantise(operand, fmt, cols, src):
+            codes, scales = operand
+            nc.vector.quantize_mx(out=codes[:, cols].bitcast(fmt), scales=scales[:, cols], in_=src)
+
+        def load_rows(src, name, cols):
+            raw = sbuf([P, PACK, cols.stop - cols.start], F32, name)
+            nc.sync.dma_start(out=raw[:], in_=src.rearrange("(p t) c -> p t c", t=PACK)[:, :, cols])
+            return raw
+
+        def load_by_row(src, name):
+            vec = sbuf([P, PACK], F32, name)
+            nc.sync.dma_start(out=vec[:], in_=src[0].rearrange("(p j) one -> p (j one)", j=PACK))
+            return vec
+
+        every = slice(0, R)
+        offsets = keep.tile([P, N // 16], U16, name="offsets")
+        scale_pool = sbuf([P, PASSES, T], U8, "scale_pool")
+        nc.vector.memset(scale_pool[:].bitcast(I32), 0)
+        q_raw = [load_rows(qT[0, 0:512], "q_raw0", every)]
+        nc.sync.dma_start(offsets[:], offs)
+        for quad in range(4):
+            nc.sync.dma_start(
+                out=scale_pool[32 * quad : 32 * quad + 4].bitcast(I32),
+                in_=c_scales[:, 4 * quad : 4 * quad + 4, :].rearrange("o f t -> f o t").bitcast(I32),
+            )
+        word_pool = sbuf([P, T], I32, "word_pool")
+        nc.sync.dma_start(out=word_pool[:], in_=c_words[0].rearrange("p t b -> p (t b)").bitcast(I32))
+        q_raw.append(load_rows(qT[0, 512:1024], "q_raw1", every))
+        lse_sb = load_by_row(lse, "lse")
+        rw_sb = load_by_row(rw, "rw")
+        delta_sb = load_by_row(delta, "delta")
+        do_raw0 = load_rows(doT[0, 0:512], "do_raw0", every)
+        do_raw1 = [load_rows(doT[0, 512:1024], "do_raw1_%d" % h, slice(256 * h, 256 * (h + 1))) for h in range(2)]
+        chunks = [slice(256 * c, 256 * (c + 1)) for c in range(4)]
+        dom_raw, qm_raw = [], []
+        for c, cols in enumerate(chunks):
+            dom_raw.append(load_rows(dom[0], "dom_raw%d" % c, cols))
+            qm_raw.append(load_rows(qm[0], "qm_raw%d" % c, cols))
+
+        windows = [sbuf([P, T], F32, "window%d" % w) for w in range(WINDOWS)]
+        for w in range(WINDOWS):
+            nc.vector.memset(windows[w][:], 0.0)
+        neg_lse = sbuf([P, PACK], F32, "neg_lse")
+        nc.gpsimd.tensor_scalar(neg_lse[:], lse_sb[:], -1.0, 0.0, ALU.mult, ALU.add)
+
+        c_planes = []
+        for o in range(PASSES):
+            plane = sbuf([P, N], U8, "c_plane%d" % o)
+            nc.vector.tensor_copy(plane[:], scale_pool[:, o, :].indirect(offsets[:]))
+            c_planes.append(plane)
+        pairs = sbuf([P, N], U32, "pairs")
+        nc.vector.tensor_copy(pairs[:], word_pool[:].bitcast(U32).indirect(offsets[:]))
+        c_codes = sbuf([P, PASSES, 2 * N], U8, "c_codes")
+        nc.vector.tensor_copy(out=c_codes[:].bitcast(U16), in_=pairs[:].bitcast(U16).rearrange("p (n o) -> p o n", o=PASSES))
+
+        def scores(bank, operand, fmt, j, o):
+            codes, scales = operand
+            cols = slice(P * j, P * (j + 1))
+            nc.tensor.matmul_mx(
+                out=bank[:], lhsT=codes[:, cols].bitcast(fmt), lhsT_scale=scales[:, cols],
+                rhs=c_codes[:, o, :].bitcast(E2M1), rhs_scale=c_planes[o][:], start=(o == 0), stop=(o == PASSES - 1),
+            )
+
+        def staging(name, tag):
+            return keep.tile([P, PACK, P, PACK], BF16, name=name, tag=tag, align_bytes=64)
+
+        q_bf = [staging("q_bf%d" % o, "staging%d" % o) for o in range(PASSES)]
+        q_mx = [quantised("q%d" % o, R) for o in range(PASSES)]
+        a_banks = [psum.tile([P, N], F32, name="a%d" % j, tag="bank%d" % j) for j in range(PACK)]
+        deal("scalar", q_bf[0][:], q_raw[0][:])
+        quantise(q_mx[0], E4M3, every, q_bf[0][:].rearrange("p j s t -> p (j s t)"))
+        for j in range(PACK):
+            scores(a_banks[j], q_mx[0], E4M3, j, 0)
+        split = 64
+        deal("vector", q_bf[1][:, :, 0:split, :], q_raw[1][:, :, 0 : 4 * split])
+        deal("scalar", q_bf[1][:, :, split:P, :], q_raw[1][:, :, 4 * split : R])
+        for half in range(2):
+            quantise(q_mx[1], E4M3, slice(256 * half, 256 * (half + 1)), q_bf[1][:, 2 * half : 2 * half + 2].rearrange("p j s t -> p (j s t)"))
+        prob = sbuf([P, PACK, N], F32, "prob")
+        pw = sbuf([P, PACK, N], F32, "pw")
+        for j in range(PACK):
+            scores(a_banks[j], q_mx[1], E4M3, j, 1)
+            nc.scalar.activation(out=prob[:, j, :], in_=a_banks[j][:], func=ACT.Exp, bias=neg_lse[:, j : j + 1], scale=1.0)
+            nc.scalar.activation(out=pw[:, j, :], in_=prob[:, j, :], func=ACT.Copy, scale=rw_sb[:, j : j + 1])
+
+        do_bf = [staging("do_bf%d" % o, "staging%d" % (1 - o)) for o in range(PASSES)]
+        do_mx = [quantised("do%d" % o, R) for o in range(PASSES)]
+        deal("vector", do_bf[0][:], do_raw0[:])
+        quantise(do_mx[0], E5M2, every, do_bf[0][:].rearrange("p j s t -> p (j s t)"))
+        dp_banks = [psum.tile([P, N], F32, name="dp%d" % j, tag="bank%d" % (PACK + j)) for j in range(PACK)]
+        for j in range(PACK):
+            scores(dp_banks[j], do_mx[0], E5M2, j, 0)
+        deal("vector", do_bf[1][:, :, 0:64, :], do_raw1[0][:])
+        deal("vector", do_bf[1][:, :, 64:P, :], do_raw1[1][:])
+        for half in range(2):
+            quantise(do_mx[1], E5M2, slice(256 * half, 256 * (half + 1)), do_bf[1][:, 2 * half : 2 * half + 2].rearrange("p j s t -> p (j s t)"))
+        pw_bf = sbuf([P, N, PACK], BF16, "pw_bf")
+        weave("scalar", pw_bf[:], pw[:])
+        ds = sbuf([P, PACK, N], F32, "ds")
+        for j in range(PACK):
+            scores(dp_banks[j], do_mx[1], E5M2, j, 1)
+            nc.vector.scalar_tensor_tensor(ds[:, j, :], dp_banks[j][:], delta_sb[:, j : j + 1], pw[:, j, :], ALU.subtract, ALU.mult)
+
+        def prepare(engine, cols, dom_tag, qm_tag):
+            c = cols.start // 256
+            width = cols.stop - cols.start
+            inside = slice(cols.start - 256 * c, cols.stop - 256 * c)
+            made = []
+            staged = []
+            for name, raw, tag in (("dom", dom_raw, dom_tag), ("qm", qm_raw, qm_tag)):
+                bf = keep.tile([P, width, PACK], BF16, name="%s_bf%d" % (name, cols.start), tag=tag, align_bytes=64)
+                weave(engine, bf[:], raw[c][:, :, inside])
+                staged.append(bf)
+            for name, fmt, bf in (("dom", E5M2, staged[0]), ("qm", E4M3, staged[1])):
+                operand = quantised("%s%d" % (name, cols.start), width)
+                quantise(operand, fmt, slice(0, width), bf[:].rearrange("p c t -> p (c t)"))
+                made.append(operand)
+            return [(made[0], made[1], slice(P * i, P * (i + 1))) for i in range(width // P)]
+
+        pw_mx, ds_mx = quantised("pw", N), quantised("ds", N)
+        quantise(pw_mx, E4M3, slice(0, N), pw_bf[:].rearrange("p n t -> p (n t)"))
+        ready = prepare("scalar", slice(0, P), "dom_first", "qm_first")
+        cut = 344
+        ds_bf = sbuf([P, N, PACK], BF16, "ds_bf")
+        weave("vector", ds_bf[:, 0:cut, :], ds[:, :, 0:cut])
+        weave("scalar", ds_bf[:, cut:N, :], ds[:, :, cut:N])
+        quantise(ds_mx, E5M2, slice(0, N), ds_bf[:].rearrange("p n t -> p (n t)"))
+        ready.extend(prepare("vector", slice(P, 2 * P), "ds_bf", "ds"))
+
+        grads = []
+        for k in range(TILES):
+            dom_mx, qm_mx, cols = ready[k]
+            bank = psum.tile([P, N], F32, name="grad%d" % k, tag="bank%d" % k)
+            nc.tensor.matmul_mx(
+                out=bank[:], lhsT=dom_mx[0][:, cols].bitcast(E5M2), lhsT_scale=dom_mx[1][:, cols],
+                rhs=pw_mx[0][:].bitcast(E4M3), rhs_scale=pw_mx[1][:], start=True, stop=False,
+            )
+            nc.tensor.matmul_mx(
+                out=bank[:], lhsT=qm_mx[0][:, cols].bitcast(E4M3), lhsT_scale=qm_mx[1][:, cols],
+                rhs=ds_mx[0][:].bitcast(E5M2), rhs_scale=ds_mx[1][:], start=False, stop=True,
+            )
+            grad = sbuf([P, N], F32, "grad_sb%d" % k)
+            grads.append(grad)
+            nc.scalar.copy(out=grad[:], in_=bank[:])
+            window = windows[k % WINDOWS]
+            nc.vector.tensor_copy(window[:].indirect(offsets[:]), grad[:])
+            nc.sync.dma_start(out=out[P * k : P * (k + 1), :], in_=window[:])
+            if k + 1 < len(chunks):
+                ready.extend(prepare("scalar", chunks[k + 1], "qm0_scales", "qm0_codes"))

@@ -37,7 +37,7 @@ def tile_attend_gat_lse_c_kernel(tc, qT, c_words, c_scales, doT, lse, delta, rw,
         copy_on(engine, dst.rearrange("p (c i) t -> p c t i", i=4), src.rearrange("p t (c i) -> p c t i", i=4))
 
     def deal(engine, dst, src):
-        copy_on(engine, dst.rearrange("p j s t -> p s t j"), src.rearrange("p t (s j) -> p s t j", j=PACK))
+        copy_on(engine, dst.rearrange("p j s t -> p s j t"), src.rearrange("p t (s j) -> p s j t", j=PACK))
 
     with ExitStack() as ctx:
         keep = ctx.enter_context(tc.tile_pool(name="keep", bufs=1))
@@ -60,7 +60,7 @@ def tile_attend_gat_lse_c_kernel(tc, qT, c_words, c_scales, doT, lse, delta, rw,
 
         def load_by_row(src, name):
             vec = sbuf([P, PACK], F32, name)
-            nc.sync.dma_start(out=vec[:], in_=src[0].rearrange("(p j) one -> p (j one)", j=PACK))
+            nc.gpsimd.dma_start(out=vec[:], in_=src[0].rearrange("(p j) one -> p (j one)", j=PACK))
             return vec
 
         every = slice(0, R)

@@ -60,31 +60,35 @@ def tile_attend_gat_lse_c_kernel(tc, qT, c_words, c_scales, doT, lse, delta, rw,
 
         def load_by_row(src, name):
             vec = sbuf([P, PACK], F32, name)
-            nc.gpsimd.dma_start(out=vec[:], in_=src[0].rearrange("(p j) one -> p (j one)", j=PACK))
+            nc.sync.dma_start(out=vec[:], in_=src[0].rearrange("(p j) one -> p (j one)", j=PACK))
             return vec
 
         every = slice(0, R)
         offsets = keep.tile([P, N // 16], U16, name="offsets")
-        scale_pool = sbuf([P, PASSES, T], U8, "scale_pool")
-        nc.vector.memset(scale_pool[:].bitcast(I32), 0)
-        q_raw = [load_rows(qT[0, 0:512], "q_raw0", every)]
         nc.sync.dma_start(offsets[:], offs)
+        word_pool = sbuf([P, T], I32, "word_pool")
+        nc.sync.dma_start(out=word_pool[:], in_=c_words[0].rearrange("p t b -> p (t b)").bitcast(I32))
+        scale_pool = sbuf([P, PASSES, T], U8, "scale_pool")
+        nc.gpsimd.memset(scale_pool[:, 0, :].bitcast(I32), 0)
+        nc.vector.memset(scale_pool[:, 1, :].bitcast(I32), 0)
         for quad in range(4):
             nc.sync.dma_start(
                 out=scale_pool[32 * quad : 32 * quad + 4].bitcast(I32),
                 in_=c_scales[:, 4 * quad : 4 * quad + 4, :].rearrange("o f t -> f o t").bitcast(I32),
             )
-        word_pool = sbuf([P, T], I32, "word_pool")
-        nc.sync.dma_start(out=word_pool[:], in_=c_words[0].rearrange("p t b -> p (t b)").bitcast(I32))
-        q_raw.append(load_rows(qT[0, 512:1024], "q_raw1", every))
         lse_sb = load_by_row(lse, "lse")
+        q_first = []
+        for h in range(2):
+            raw = sbuf([P, 2, R], F32, "q_raw0_%d" % h)
+            nc.sync.dma_start(out=raw[:], in_=qT[0, 0:512].rearrange("(p t) c -> p t c", t=PACK)[:, 2 * h : 2 * h + 2, :])
+            q_first.append(raw)
         rw_sb = load_by_row(rw, "rw")
         delta_sb = load_by_row(delta, "delta")
-        do_raw0 = load_rows(doT[0, 0:512], "do_raw0", every)
-        do_raw1 = [load_rows(doT[0, 512:1024], "do_raw1_%d" % h, slice(256 * h, 256 * (h + 1))) for h in range(2)]
+        q_second = load_rows(qT[0, 512:1024], "q_raw1", every)
+        do_raw = [load_rows(doT[0, 512 * o : 512 * (o + 1)], "do_raw%d" % o, every) for o in range(PASSES)]
         chunks = [slice(256 * c, 256 * (c + 1)) for c in range(4)]
         dom_raw, qm_raw = [], []
-        for c, cols in enumerate(chunks):
+        for c, cols in enumerate((slice(0, 256), slice(256, 512), slice(512, D))):
             dom_raw.append(load_rows(dom[0], "dom_raw%d" % c, cols))
             qm_raw.append(load_rows(qm[0], "qm_raw%d" % c, cols))
 
@@ -92,17 +96,17 @@ def tile_attend_gat_lse_c_kernel(tc, qT, c_words, c_scales, doT, lse, delta, rw,
         for w in range(WINDOWS):
             nc.vector.memset(windows[w][:], 0.0)
         neg_lse = sbuf([P, PACK], F32, "neg_lse")
-        nc.gpsimd.tensor_scalar(neg_lse[:], lse_sb[:], -1.0, 0.0, ALU.mult, ALU.add)
+        nc.vector.tensor_scalar(neg_lse[:], lse_sb[:], -1.0, None, ALU.mult)
 
+        pairs = sbuf([P, N], U32, "pairs")
+        nc.vector.tensor_copy(pairs[:], word_pool[:].bitcast(U32).indirect(offsets[:]))
+        c_codes = sbuf([P, PASSES, 2 * N], U8, "c_codes")
+        nc.vector.tensor_copy(out=c_codes[:].bitcast(U16), in_=pairs[:].bitcast(U16).rearrange("p (n o) -> p o n", o=PASSES))
         c_planes = []
         for o in range(PASSES):
             plane = sbuf([P, N], U8, "c_plane%d" % o)
             nc.vector.tensor_copy(plane[:], scale_pool[:, o, :].indirect(offsets[:]))
             c_planes.append(plane)
-        pairs = sbuf([P, N], U32, "pairs")
-        nc.vector.tensor_copy(pairs[:], word_pool[:].bitcast(U32).indirect(offsets[:]))
-        c_codes = sbuf([P, PASSES, 2 * N], U8, "c_codes")
-        nc.vector.tensor_copy(out=c_codes[:].bitcast(U16), in_=pairs[:].bitcast(U16).rearrange("p (n o) -> p o n", o=PASSES))
 
         def scores(bank, operand, fmt, j, o):
             codes, scales = operand
@@ -118,31 +122,33 @@ def tile_attend_gat_lse_c_kernel(tc, qT, c_words, c_scales, doT, lse, delta, rw,
         q_bf = [staging("q_bf%d" % o, "staging%d" % o) for o in range(PASSES)]
         q_mx = [quantised("q%d" % o, R) for o in range(PASSES)]
         a_banks = [psum.tile([P, N], F32, name="a%d" % j, tag="bank%d" % j) for j in range(PACK)]
-        deal("scalar", q_bf[0][:], q_raw[0][:])
+        for h in range(2):
+            deal("scalar", q_bf[0][:, :, :, 2 * h : 2 * h + 2], q_first[h][:])
         quantise(q_mx[0], E4M3, every, q_bf[0][:].rearrange("p j s t -> p (j s t)"))
-        for j in range(PACK):
-            scores(a_banks[j], q_mx[0], E4M3, j, 0)
-        split = 64
-        deal("vector", q_bf[1][:, :, 0:split, :], q_raw[1][:, :, 0 : 4 * split])
-        deal("scalar", q_bf[1][:, :, split:P, :], q_raw[1][:, :, 4 * split : R])
+        split = 80
+        deal("vector", q_bf[1][:, :, 0:split, :], q_second[:, :, 0 : 4 * split])
+        deal("scalar", q_bf[1][:, :, split:P, :], q_second[:, :, 4 * split : R])
         for half in range(2):
             quantise(q_mx[1], E4M3, slice(256 * half, 256 * (half + 1)), q_bf[1][:, 2 * half : 2 * half + 2].rearrange("p j s t -> p (j s t)"))
+        do_bf = [staging("do_bf%d" % o, "staging%d" % (1 - o)) for o in range(PASSES)]
+        do_mx = [quantised("do%d" % o, R) for o in range(PASSES)]
+        deal("vector", do_bf[0][:], do_raw[0][:])
         prob = sbuf([P, PACK, N], F32, "prob")
         pw = sbuf([P, PACK, N], F32, "pw")
         for j in range(PACK):
-            scores(a_banks[j], q_mx[1], E4M3, j, 1)
+            for o in range(PASSES):
+                scores(a_banks[j], q_mx[o], E4M3, j, o)
             nc.scalar.activation(out=prob[:, j, :], in_=a_banks[j][:], func=ACT.Exp, bias=neg_lse[:, j : j + 1], scale=1.0)
+        for j in range(2, PACK):
             nc.scalar.activation(out=pw[:, j, :], in_=prob[:, j, :], func=ACT.Copy, scale=rw_sb[:, j : j + 1])
 
-        do_bf = [staging("do_bf%d" % o, "staging%d" % (1 - o)) for o in range(PASSES)]
-        do_mx = [quantised("do%d" % o, R) for o in range(PASSES)]
-        deal("vector", do_bf[0][:], do_raw0[:])
+        for j in range(2):
+            nc.vector.tensor_scalar(pw[:, j, :], prob[:, j, :], rw_sb[:, j : j + 1], None, ALU.mult)
         quantise(do_mx[0], E5M2, every, do_bf[0][:].rearrange("p j s t -> p (j s t)"))
         dp_banks = [psum.tile([P, N], F32, name="dp%d" % j, tag="bank%d" % (PACK + j)) for j in range(PACK)]
         for j in range(PACK):
             scores(dp_banks[j], do_mx[0], E5M2, j, 0)
-        deal("vector", do_bf[1][:, :, 0:64, :], do_raw1[0][:])
-        deal("vector", do_bf[1][:, :, 64:P, :], do_raw1[1][:])
+        deal("vector", do_bf[1][:], do_raw[1][:])
         for half in range(2):
             quantise(do_mx[1], E5M2, slice(256 * half, 256 * (half + 1)), do_bf[1][:, 2 * half : 2 * half + 2].rearrange("p j s t -> p (j s t)"))
         pw_bf = sbuf([P, N, PACK], BF16, "pw_bf")
@@ -153,7 +159,7 @@ def tile_attend_gat_lse_c_kernel(tc, qT, c_words, c_scales, doT, lse, delta, rw,
             nc.vector.scalar_tensor_tensor(ds[:, j, :], dp_banks[j][:], delta_sb[:, j : j + 1], pw[:, j, :], ALU.subtract, ALU.mult)
 
         def prepare(engine, cols, dom_tag, qm_tag):
-            c = cols.start // 256
+            c = min(cols.start // 256, 2)
             width = cols.stop - cols.start
             inside = slice(cols.start - 256 * c, cols.stop - 256 * c)
             made = []
@@ -169,12 +175,12 @@ def tile_attend_gat_lse_c_kernel(tc, qT, c_words, c_scales, doT, lse, delta, rw,
             return [(made[0], made[1], slice(P * i, P * (i + 1))) for i in range(width // P)]
 
         pw_mx, ds_mx = quantised("pw", N), quantised("ds", N)
-        quantise(pw_mx, E4M3, slice(0, N), pw_bf[:].rearrange("p n t -> p (n t)"))
-        ready = prepare("scalar", slice(0, P), "dom_first", "qm_first")
-        cut = 344
         ds_bf = sbuf([P, N, PACK], BF16, "ds_bf")
+        cut = 192
         weave("vector", ds_bf[:, 0:cut, :], ds[:, :, 0:cut])
+        ready = prepare("scalar", slice(0, P), "dom_first", "qm_first")
         weave("scalar", ds_bf[:, cut:N, :], ds[:, :, cut:N])
+        quantise(pw_mx, E4M3, slice(0, N), pw_bf[:].rearrange("p n t -> p (n t)"))
         quantise(ds_mx, E5M2, slice(0, N), ds_bf[:].rearrange("p n t -> p (n t)"))
         ready.extend(prepare("vector", slice(P, 2 * P), "ds_bf", "ds"))
 
@@ -197,4 +203,4 @@ def tile_attend_gat_lse_c_kernel(tc, qT, c_words, c_scales, doT, lse, delta, rw,
             nc.vector.tensor_copy(window[:].indirect(offsets[:]), grad[:])
             nc.sync.dma_start(out=out[P * k : P * (k + 1), :], in_=window[:])
             if k + 1 < len(chunks):
-                ready.extend(prepare("scalar", chunks[k + 1], "qm0_scales", "qm0_codes"))
+                ready.extend(prepare("scalar", chunks[k + 1], "qm%d_scales" % (P * (k % 2)), "qm%d_codes" % (P * (k % 2))))

from contextlib import ExitStack

import concourse.mybir as mybir

N, T, D, R = 512, 2048, 1024, 512
FLOPS = 4 * 2 * R * N * D

F32 = mybir.dt.float32
BF16 = mybir.dt.bfloat16
I32 = mybir.dt.int32
U32 = mybir.dt.uint32
U16 = mybir.dt.uint16
U8 = mybir.dt.uint8
E4M3 = mybir.dt.float8_e4m3fn_x4
E5M2 = mybir.dt.float8_e5m2_x4
E2M1 = mybir.dt.float4_e2m1fn_x4
ALU = mybir.AluOpType
ACT = mybir.ActivationFunctionType

P = 128
PACK = 4
PASSES = D // (P * PACK)
TILES = D // P
WINDOWS = 3


def tile_attend_gat_lse_c_kernel(tc, qT, c_words, c_scales, doT, lse, delta, rw, qm, dom, offs, out):
    nc = tc.nc

    def copy_on(engine, dst, src):
        if engine == "vector":
            nc.vector.tensor_copy(out=dst, in_=src)
        else:
            nc.scalar.copy(out=dst, in_=src)

    def weave(engine, dst, src):
        copy_on(engine, dst.rearrange("p (c i) t -> p c t i", i=4), src.rearrange("p t (c i) -> p c t i", i=4))

    def deal(engine, dst, src):
        copy_on(engine, dst.rearrange("p j s t -> p s j t"), src.rearrange("p t (s j) -> p s j t", j=PACK))

    with ExitStack() as ctx:
        keep = ctx.enter_context(tc.tile_pool(name="keep", bufs=1))
        psum = ctx.enter_context(tc.psum_pool(name="psum", bufs=1))

        def sbuf(shape, dtype, name):
            return keep.tile(shape, dtype, name=name, align_bytes=64)

        def quantised(name, width):
            return sbuf([P, width], U32, name + "_codes"), sbuf([P, width], U8, name + "_scales")

        def quantise(operand, fmt, cols, src):
            codes, scales = operand
            nc.vector.quantize_mx(out=codes[:, cols].bitcast(fmt), scales=scales[:, cols], in_=src)

        def load_rows(src, name, cols):
            raw = sbuf([P, PACK, cols.stop - cols.start], F32, name)
            nc.sync.dma_start(out=raw[:], in_=src.rearrange("(p t) c -> p t c", t=PACK)[:, :, cols])
            return raw

        def load_by_row(src, name):
            vec = sbuf([P, PACK], F32, name)
            nc.sync.dma_start(out=vec[:], in_=src[0].rearrange("(p j) one -> p (j one)", j=PACK))
            return vec

        every = slice(0, R)
        offsets = keep.tile([P, N // 16], U16, name="offsets")
        nc.sync.dma_start(offsets[:], offs)
        word_pool = sbuf([P, T], I32, "word_pool")
        nc.sync.dma_start(out=word_pool[:], in_=c_words[0].rearrange("p t b -> p (t b)").bitcast(I32))
        scale_pool = sbuf([P, PASSES, T], U8, "scale_pool")
        nc.gpsimd.memset(scale_pool[:, 0, :].bitcast(I32), 0)
        nc.vector.memset(scale_pool[:, 1, :].bitcast(I32), 0)
        for quad in range(4):
            nc.sync.dma_start(
                out=scale_pool[32 * quad : 32 * quad + 4].bitcast(I32),
                in_=c_scales[:, 4 * quad : 4 * quad + 4, :].rearrange("o f t -> f o t").bitcast(I32),
            )
        lse_sb = load_by_row(lse, "lse")
        q_first = []
        for h in range(2):
            raw = sbuf([P, 2, R], F32, "q_raw0_%d" % h)
            nc.sync.dma_start(out=raw[:], in_=qT[0, 0:512].rearrange("(p t) c -> p t c", t=PACK)[:, 2 * h : 2 * h + 2, :])
            q_first.append(raw)
        rw_sb = load_by_row(rw, "rw")
        delta_sb = load_by_row(delta, "delta")
        q_second = load_rows(qT[0, 512:1024], "q_raw1", every)
        do_raw = [load_rows(doT[0, 512 * o : 512 * (o + 1)], "do_raw%d" % o, every) for o in range(PASSES)]
        chunks = [slice(256 * c, 256 * (c + 1)) for c in range(4)]
        dom_raw, qm_raw = [], []
        for c, cols in enumerate((slice(0, 256), slice(256, 512), slice(512, D))):
            dom_raw.append(load_rows(dom[0], "dom_raw%d" % c, cols))
            qm_raw.append(load_rows(qm[0], "qm_raw%d" % c, cols))

        windows = [sbuf([P, T], F32, "window%d" % w) for w in range(WINDOWS)]
        for w in range(WINDOWS):
            nc.vector.memset(windows[w][:], 0.0)
        neg_lse = sbuf([P, PACK], F32, "neg_lse")
        nc.vector.tensor_scalar(neg_lse[:], lse_sb[:], -1.0, None, ALU.mult)

        pairs = sbuf([P, N], U32, "pairs")
        nc.vector.tensor_copy(pairs[:], word_pool[:].bitcast(U32).indirect(offsets[:]))
        c_codes = sbuf([P, PASSES, 2 * N], U8, "c_codes")
        nc.vector.tensor_copy(out=c_codes[:].bitcast(U16), in_=pairs[:].bitcast(U16).rearrange("p (n o) -> p o n", o=PASSES))
        c_planes = []
        for o in range(PASSES):
            plane = sbuf([P, N], U8, "c_plane%d" % o)
            nc.vector.tensor_copy(plane[:], scale_pool[:, o, :].indirect(offsets[:]))
            c_planes.append(plane)

        def scores(bank, operand, fmt, j, o):
            codes, scales = operand
            cols = slice(P * j, P * (j + 1))
            nc.tensor.matmul_mx(
                out=bank[:], lhsT=codes[:, cols].bitcast(fmt), lhsT_scale=scales[:, cols],
                rhs=c_codes[:, o, :].bitcast(E2M1), rhs_scale=c_planes[o][:], start=(o == 0), stop=(o == PASSES - 1),
            )

        def staging(name, tag):
            return keep.tile([P, PACK, P, PACK], BF16, name=name, tag=tag, align_bytes=64)

        q_bf = [staging("q_bf%d" % o, "staging%d" % o) for o in range(PASSES)]
        q_mx = [quantised("q%d" % o, R) for o in range(PASSES)]
        a_banks = [psum.tile([P, N], F32, name="a%d" % j, tag="bank%d" % j) for j in range(PACK)]
        for h in range(2):
            deal("scalar", q_bf[0][:, :, :, 2 * h : 2 * h + 2], q_first[h][:])
        quantise(q_mx[0], E4M3, every, q_bf[0][:].rearrange("p j s t -> p (j s t)"))
        split = 80
        deal("vector", q_bf[1][:, :, 0:split, :], q_second[:, :, 0 : 4 * split])
        deal("scalar", q_bf[1][:, :, split:P, :], q_second[:, :, 4 * split : R])
        for half in range(2):
            quantise(q_mx[1], E4M3, slice(256 * half, 256 * (half + 1)), q_bf[1][:, 2 * half : 2 * half + 2].rearrange("p j s t -> p (j s t)"))
        do_bf = [staging("do_bf%d" % o, "staging%d" % (1 - o)) for o in range(PASSES)]
        do_mx = [quantised("do%d" % o, R) for o in range(PASSES)]
        deal("vector", do_bf[0][:], do_raw[0][:])
        prob = sbuf([P, PACK, N], F32, "prob")
        pw = sbuf([P, PACK, N], F32, "pw")
        for j in range(PACK):
            for o in range(PASSES):
                scores(a_banks[j], q_mx[o], E4M3, j, o)
            nc.scalar.activation(out=prob[:, j, :], in_=a_banks[j][:], func=ACT.Exp, bias=neg_lse[:, j : j + 1], scale=1.0)
        for j in range(2, PACK):
            nc.scalar.activation(out=pw[:, j, :], in_=prob[:, j, :], func=ACT.Copy, scale=rw_sb[:, j : j + 1])

        for j in range(2):
            nc.vector.tensor_scalar(pw[:, j, :], prob[:, j, :], rw_sb[:, j : j + 1], None, ALU.mult)
        quantise(do_mx[0], E5M2, every, do_bf[0][:].rearrange("p j s t -> p (j s t)"))
        dp_banks = [psum.tile([P, N], F32, name="dp%d" % j, tag="bank%d" % (PACK + j)) for j in range(PACK)]
        for j in range(PACK):
            scores(dp_banks[j], do_mx[0], E5M2, j, 0)
        deal("vector", do_bf[1][:], do_raw[1][:])
        for half in range(2):
            quantise(do_mx[1], E5M2, slice(256 * half, 256 * (half + 1)), do_bf[1][:, 2 * half : 2 * half + 2].rearrange("p j s t -> p (j s t)"))
        pw_bf = sbuf([P, N, PACK], BF16, "pw_bf")
        weave("scalar", pw_bf[:], pw[:])
        ds = sbuf([P, PACK, N], F32, "ds")
        for j in range(PACK):
            scores(dp_banks[j], do_mx[1], E5M2, j, 1)
            nc.vector.scalar_tensor_tensor(ds[:, j, :], dp_banks[j][:], delta_sb[:, j : j + 1], pw[:, j, :], ALU.subtract, ALU.mult)

        def prepare(engine, cols, dom_tag, qm_tag):
            c = min(cols.start // 256, 2)
            width = cols.stop - cols.start
            inside = slice(cols.start - 256 * c, cols.stop - 256 * c)
            made = []
            staged = []
            for name, raw, tag in (("dom", dom_raw, dom_tag), ("qm", qm_raw, qm_tag)):
                bf = keep.tile([P, width, PACK], BF16, name="%s_bf%d" % (name, cols.start), tag=tag, align_bytes=64)
                weave(engine, bf[:], raw[c][:, :, inside])
                staged.append(bf)
            for name, fmt, bf in (("dom", E5M2, staged[0]), ("qm", E4M3, staged[1])):
                operand = quantised("%s%d" % (name, cols.start), width)
                quantise(operand, fmt, slice(0, width), bf[:].rearrange("p c t -> p (c t)"))
                made.append(operand)
            return [(made[0], made[1], slice(P * i, P * (i + 1))) for i in range(width // P)]

        pw_mx, ds_mx = quantised("pw", N), quantised("ds", N)
        ds_bf = sbuf([P, N, PACK], BF16, "ds_bf")
        cut = 192
        weave("vector", ds_bf[:, 0:cut, :], ds[:, :, 0:cut])
        ready = prepare("scalar", slice(0, P), "dom_first", "qm_first")
        weave("scalar", ds_bf[:, cut:N, :], ds[:, :, cut:N])
        quantise(pw_mx, E4M3, slice(0, N), pw_bf[:].rearrange("p n t -> p (n t)"))
        quantise(ds_mx, E5M2, slice(0, N), ds_bf[:].rearrange("p n t -> p (n t)"))
        ready.extend(prepare("vector", slice(P, 2 * P), "ds_bf", "ds"))

        grads = []
        for k in range(TILES):
            dom_mx, qm_mx, cols = ready[k]
            bank = psum.tile([P, N], F32, name="grad%d" % k, tag="bank%d" % k)
            nc.tensor.matmul_mx(
                out=bank[:], lhsT=dom_mx[0][:, cols].bitcast(E5M2), lhsT_scale=dom_mx[1][:, cols],
                rhs=pw_mx[0][:].bitcast(E4M3), rhs_scale=pw_mx[1][:], start=True, stop=False,
            )
            nc.tensor.matmul_mx(
                out=bank[:], lhsT=qm_mx[0][:, cols].bitcast(E4M3), lhsT_scale=qm_mx[1][:, cols],
                rhs=ds_mx[0][:].bitcast(E5M2), rhs_scale=ds_mx[1][:], start=False, stop=True,
            )
            grad = sbuf([P, N], F32, "grad_sb%d" % k)
            grads.append(grad)
            nc.scalar.copy(out=grad[:], in_=bank[:])
            window = windows[k % WINDOWS]
            nc.vector.tensor_copy(window[:].indirect(offsets[:]), grad[:])
            nc.sync.dma_start(out=out[P * k : P * (k + 1), :], in_=window[:])
            if k + 1 < len(chunks):
                ready.extend(prepare("scalar", chunks[k + 1], "qm%d_scales" % (P * (k % 2)), "qm%d_codes" % (P * (k % 2))))
